import numpy as np
import ml_dtypes


def mxq(x, axis, fmt="e4m3"):
    dtype, down = {"e4m3": (ml_dtypes.float8_e4m3fn, 7), "e5m2": (ml_dtypes.float8_e5m2, 14)}[fmt]
    v = np.moveaxis(np.asarray(x, np.float32).astype(ml_dtypes.bfloat16).astype(np.float64), axis, -1)
    blocks = v.reshape(v.shape[:-1] + (-1, 32))
    amax = np.abs(blocks).max(-1, keepdims=True)
    byte = np.maximum(np.where(amax > 0, np.frexp(amax)[1] - 1 + 127, 0) - down, 1)
    scale = np.exp2(byte - 127.0)
    codes = (blocks / scale).astype(np.float32).astype(dtype).astype(np.float64)
    return np.moveaxis((codes * scale).reshape(v.shape), -1, axis)


WIDE = False


def mx_kscale(k):
    if not WIDE:
        return np.ones(k)
    levels = np.array([10, -10, 5, -5, 0])
    if k % 512:
        return np.exp2(np.random.permutation(np.resize(levels, k // 32))).repeat(32)
    a = np.empty((k // 512, 16))
    for p in range(k // 512):
        a[p, :8] = np.random.permutation(np.resize(levels, 8))
        for g in range(8):
            far = levels[np.abs(levels - a[p, g]) >= 10]
            a[p, g + 8] = far[np.random.randint(len(far))]
    return np.exp2(a.ravel()).repeat(32)


def f64(x):
    return np.asarray(x).astype(np.float64)


def striped8(idx):
    return np.asarray(idx).reshape(8, -1, 16).transpose(0, 2, 1).reshape(128, -1).astype(np.uint16)


def unstriped8(offs):
    return offs.reshape(8, 16, -1).transpose(0, 2, 1).reshape(8, -1).astype(np.int64)


def pick8(x, idx, run):
    r = np.arange(len(x))
    return x[r[:, None], idx[r % (8 * run) // run]]


E2M1 = np.array([0.0, 0.5, 1.0, 1.5, 2.0, 3.0, 4.0, 6.0, -0.0, -0.5, -1.0, -1.5, -2.0, -3.0, -4.0, -6.0])


def pack_weight(w, fmt):
    k, n = w.shape
    w = f64(np.asarray(w, np.float32).astype(ml_dtypes.bfloat16)).reshape(k // 32, 32, n)
    amax = np.abs(w).max(1)
    if fmt == "e4m3":
        byte = np.frexp(amax)[1] - 1 + 127 - 7
    else:
        mant, ex = np.frexp(amax / 6.0)
        byte = np.where(mant > 0.5, ex, ex - 1) + 127
    byte = np.clip(np.where(amax > 0, byte, 1), 1, 254)
    scaled = (w * np.exp2(127.0 - byte)[:, None, :]).reshape(k, n).astype(np.float32)
    by_word = np.ascontiguousarray(scaled.reshape(k // 512, 128, 4, n).transpose(0, 1, 3, 2))
    if fmt == "e4m3":
        words = by_word.astype(ml_dtypes.float8_e4m3fn).view(np.uint8)
    else:
        c = by_word.astype(ml_dtypes.float4_e2m1fn).view(np.uint8) & 0xF
        words = (c[..., 0::2] | (c[..., 1::2] << 4)).reshape(k // 512, 128, 2 * n)
    return np.ascontiguousarray(words), np.ascontiguousarray(byte.astype(np.uint8).reshape(k // 512, 16, n))


def unpack_weight(words, scales, fmt):
    g, _, n = scales.shape
    words = np.ascontiguousarray(words).reshape(g, 128, n, -1)
    if fmt == "e4m3":
        vals = words.view(ml_dtypes.float8_e4m3fn).astype(np.float64)
    else:
        nib = np.empty((g, 128, n, 4), np.uint8)
        nib[..., 0::2] = words & 0xF
        nib[..., 1::2] = words >> 4
        vals = E2M1[nib]
    vals = vals * np.repeat(np.exp2(scales.astype(np.float64) - 127.0), 8, axis=1)[..., None]
    return vals.transpose(0, 1, 3, 2).reshape(g * 512, n)


D, T, I, Q = 512, 1024, 512, 128


def setup_inputs():
    n = np.random.standard_normal
    idx = np.stack([np.random.permutation(T)[:I] for _ in range(8)])
    idx2 = np.stack([np.random.permutation(T)[:I] for _ in range(8)])
    idx3 = np.stack([np.random.permutation(T)[:I] for _ in range(8)])
    idx4 = np.stack([np.random.permutation(T)[:I] for _ in range(8)])
    fd = mx_kscale(D)
    keysp = pack_weight(n((D, T)) / fd[:, None], "e2m1")
    return {
        "query": (n((D, Q)) * 1.0 / np.sqrt(D) * fd[:, None]).astype(np.float32),
        "keys_words": keysp[0],
        "keys_scales": keysp[1],
        "old": (np.random.uniform(0.3, 1.7, (Q, T))).astype(np.float32),
        "base": (0.5 * n((Q, T))).astype(np.float32),
        "offs": striped8(idx),
        "offs2": striped8(idx2),
        "offs3": striped8(idx3),
        "offs4": striped8(idx4),
    }


def reference(query, keys_words, keys_scales, old, base, offs, offs2, offs3, offs4):
    idx = unstriped8(offs)
    idx2 = unstriped8(offs2)
    idx3 = unstriped8(offs3)
    idx4 = unstriped8(offs4)
    keysu = unpack_weight(keys_words, keys_scales, "e2m1")
    queryq = mxq(f64(query), 0, "e4m3")
    a = queryq.T @ keysu
    w = pick8(a, idx, 16) * pick8(a, idx2, 16)
    ws = w * pick8(f64(old), idx3, 16)
    f1 = np.zeros((Q, T))
    f1[np.arange(Q)[:, None], idx4[np.arange(Q) % 128 // 16]] = ws
    y = f64(base) + f1
    return y

@@ -1,0 +1,115 @@
+from contextlib import ExitStack
+
+import concourse.mybir as mybir
+
+D, T, I, Q = 512, 1024, 512, 128
+FLOPS = 2 * D * T * Q
+
+F32 = mybir.dt.float32
+BF16 = mybir.dt.bfloat16
+U32 = mybir.dt.uint32
+I32 = mybir.dt.int32
+U16 = mybir.dt.uint16
+U8 = mybir.dt.uint8
+FP8X4 = mybir.dt.float8_e4m3fn_x4
+FP4X4 = mybir.dt.float4_e2m1fn_x4
+MULT = mybir.AluOpType.mult
+ADD = mybir.AluOpType.add
+COPY = mybir.ActivationFunctionType.Copy
+
+P = 128
+PACK = 4
+N_MM = 256
+HALF = I // 2
+N_OUT = 256
+
+
+def tile_attend_pairproduct_lean_timesold_heads_kernel(
+    tc, query, keys_words, keys_scales, old, base, offs, offs2, offs3, offs4, out
+):
+    nc = tc.nc
+    with ExitStack() as ctx:
+        keep = ctx.enter_context(tc.tile_pool(name="keep", bufs=1))
+        psum = ctx.enter_context(tc.psum_pool(name="psum", bufs=1))
+
+        lst1 = keep.tile([P, I // 16], U16, name="lst1")
+        lst2 = keep.tile([P, I // 16], U16, name="lst2")
+        lst3 = keep.tile([P, I // 16], U16, name="lst3")
+        lst4 = keep.tile([P, I // 16], U16, name="lst4")
+        q_raw = keep.tile([P, PACK, Q], F32, name="q_raw")
+        k_words = keep.tile([P, 2 * T], U8, name="k_words", align_bytes=64)
+        k_scales = keep.tile([P, T], U8, name="k_scales", align_bytes=64)
+        old_sb = keep.tile([P, T], F32, name="old_sb")
+        base_sb = keep.tile([P, T], F32, name="base_sb")
+        f1 = keep.tile([P, T], F32, name="f1")
+        a_sb = keep.tile([P, T], F32, name="a_sb")
+
+        nc.vector.memset(k_scales[:].bitcast(I32), 0)
+        nc.sync.dma_start(q_raw[:], query.rearrange("(p j) q -> p j q", j=PACK))
+        nc.sync.dma_start(k_words[:].bitcast(I32), keys_words[0].bitcast(I32))
+        for quad in range(4):
+            nc.sync.dma_start(
+                k_scales[32 * quad : 32 * quad + 4, :].bitcast(I32),
+                keys_scales[0, 4 * quad : 4 * quad + 4, :].bitcast(I32),
+            )
+        nc.sync.dma_start(lst3[:], offs3)
+        nc.sync.dma_start(old_sb[:], old)
+        nc.sync.dma_start(lst1[:], offs)
+        nc.sync.dma_start(lst2[:], offs2)
+        nc.sync.dma_start(lst4[:], offs4)
+        nc.sync.dma_start(base_sb[:], base)
+        nc.vector.memset(f1[:], 0.0)
+
+        q_bf = keep.tile([P, Q, PACK], BF16, name="q_bf", align_bytes=64)
+        nc.vector.tensor_copy(
+            q_bf[:].rearrange("p (c i) t -> p c t i", i=4),
+            q_raw[:].rearrange("p t (c i) -> p c t i", i=4),
+        )
+        q_codes = keep.tile([P, Q], U32, name="q_codes", align_bytes=64)
+        q_scales = keep.tile([P, Q], U8, name="q_scales", align_bytes=64)
+        nc.vector.quantize_mx(
+            out=q_codes[:].bitcast(FP8X4),
+            scales=q_scales[:],
+            in_=q_bf[:].rearrange("p c t -> p (c t)"),
+        )
+
+        for c in range(T // N_MM):
+            bank = psum.tile([P, N_MM], F32, name="bank%d" % c)
+            nc.tensor.matmul_mx(
+                out=bank[:],
+                lhsT=q_codes[:].bitcast(FP8X4),
+                lhsT_scale=q_scales[:],
+                rhs=k_words[:, 2 * N_MM * c : 2 * N_MM * (c + 1)].bitcast(FP4X4),
+                rhs_scale=k_scales[:, N_MM * c : N_MM * (c + 1)],
+                start=True,
+                stop=True,
+            )
+            nc.vector.tensor_copy(a_sb[:, N_MM * c : N_MM * (c + 1)], bank[:])
+
+        first = slice(0, HALF // 16)
+        second = slice(HALF // 16, I // 16)
+        old_0 = keep.tile([P, HALF], F32, name="old_0", tag="old_picked")
+        a2_0 = keep.tile([P, HALF], F32, name="a2_0")
+        a1o_0 = keep.tile([P, HALF], F32, name="a1o_0")
+        a1_1 = keep.tile([P, HALF], F32, name="a1_1")
+        a2_1 = keep.tile([P, HALF], F32, name="a2_1")
+        a1o_1 = keep.tile([P, HALF], F32, name="a1o_1")
+
+        nc.scalar.activation(old_0[:], old_sb[:].indirect(lst3[:, first]), COPY)
+        nc.scalar.activation(a2_0[:], a_sb[:].indirect(lst2[:, first]), COPY)
+        nc.vector.tensor_tensor(a1o_0[:], a_sb[:].indirect(lst1[:, first]), old_0[:], MULT)
+        nc.vector.tensor_tensor(f1[:].indirect(lst4[:, first]), a1o_0[:], a2_0[:], MULT)
+
+        old_1 = keep.tile([P, HALF], F32, name="old_1", tag="old_picked")
+        nc.scalar.activation(old_1[:], old_sb[:].indirect(lst3[:, second]), COPY)
+        nc.scalar.activation(a1_1[:], a_sb[:].indirect(lst1[:, second]), COPY)
+        nc.scalar.activation(a2_1[:], a_sb[:].indirect(lst2[:, second]), COPY)
+        nc.vector.tensor_tensor(a1o_1[:], a1_1[:], old_1[:], MULT)
+        nc.vector.tensor_tensor(f1[:].indirect(lst4[:, second]), a1o_1[:], a2_1[:], MULT)
+
+        for c in range(T // N_OUT):
+            cols = slice(N_OUT * c, N_OUT * (c + 1))
+            res = keep.tile([P, N_OUT], F32, name="res%d" % c)
+            nc.vector.tensor_tensor(res[:], base_sb[:, cols], f1[:, cols], ADD)
+            queue = nc.sync if c % 2 == 0 else nc.scalar
+            queue.dma_start(out[:, cols], res[:])

@@ -22,6 +22,7 @@ PACK = 4
 N_MM = 256
 HALF = I // 2
 N_OUT = 256
+LEAD = 128
 
 
 def tile_attend_pairproduct_lean_timesold_heads_kernel(
@@ -84,28 +85,28 @@ def tile_attend_pairproduct_lean_timesold_heads_kernel(
                 start=True,
                 stop=True,
             )
-            nc.vector.tensor_copy(a_sb[:, N_MM * c : N_MM * (c + 1)], bank[:])
+            nc.scalar.copy(a_sb[:, N_MM * c : N_MM * (c + 1)], bank[:])
 
-        first = slice(0, HALF // 16)
-        second = slice(HALF // 16, I // 16)
-        old_0 = keep.tile([P, HALF], F32, name="old_0", tag="old_picked")
-        a2_0 = keep.tile([P, HALF], F32, name="a2_0")
-        a1o_0 = keep.tile([P, HALF], F32, name="a1o_0")
-        a1_1 = keep.tile([P, HALF], F32, name="a1_1")
-        a2_1 = keep.tile([P, HALF], F32, name="a2_1")
-        a1o_1 = keep.tile([P, HALF], F32, name="a1o_1")
+        def slots(lo, hi):
+            return slice(lo // 16, hi // 16)
 
-        nc.scalar.activation(old_0[:], old_sb[:].indirect(lst3[:, first]), COPY)
-        nc.scalar.activation(a2_0[:], a_sb[:].indirect(lst2[:, first]), COPY)
-        nc.vector.tensor_tensor(a1o_0[:], a_sb[:].indirect(lst1[:, first]), old_0[:], MULT)
-        nc.vector.tensor_tensor(f1[:].indirect(lst4[:, first]), a1o_0[:], a2_0[:], MULT)
+        old_g = keep.tile([P, I], F32, name="old_g")
+        a2_g = keep.tile([P, I], F32, name="a2_g")
+        a1_g = keep.tile([P, HALF], F32, name="a1_g")
+        a1o = keep.tile([P, I], F32, name="a1o")
 
-        old_1 = keep.tile([P, HALF], F32, name="old_1", tag="old_picked")
-        nc.scalar.activation(old_1[:], old_sb[:].indirect(lst3[:, second]), COPY)
-        nc.scalar.activation(a1_1[:], a_sb[:].indirect(lst1[:, second]), COPY)
-        nc.scalar.activation(a2_1[:], a_sb[:].indirect(lst2[:, second]), COPY)
-        nc.vector.tensor_tensor(a1o_1[:], a1_1[:], old_1[:], MULT)
-        nc.vector.tensor_tensor(f1[:].indirect(lst4[:, second]), a1o_1[:], a2_1[:], MULT)
+        for lo in (0, HALF):
+            nc.vector.tensor_copy(old_g[:, lo : lo + HALF], old_sb[:].indirect(lst3[:, slots(lo, lo + HALF)]))
+        nc.scalar.activation(a2_g[:, 0:HALF], a_sb[:].indirect(lst2[:, slots(0, HALF)]), COPY)
+        nc.scalar.activation(a1_g[:], a_sb[:].indirect(lst1[:, slots(HALF, I)]), COPY)
+        nc.scalar.activation(a2_g[:, HALF:I], a_sb[:].indirect(lst2[:, slots(HALF, I)]), COPY)
+        for lo in (0, LEAD):
+            nc.vector.tensor_tensor(
+                a1o[:, lo : lo + LEAD], a_sb[:].indirect(lst1[:, slots(lo, lo + LEAD)]), old_g[:, lo : lo + LEAD], MULT
+            )
+        nc.vector.tensor_tensor(f1[:].indirect(lst4[:, slots(0, LEAD)]), a1o[:, 0:LEAD], a2_g[:, 0:LEAD], MULT)
+        nc.vector.tensor_tensor(a1o[:, HALF:I], a1_g[:], old_g[:, HALF:I], MULT)
+        nc.vector.tensor_tensor(f1[:].indirect(lst4[:, slots(LEAD, I)]), a1o[:, LEAD:I], a2_g[:, LEAD:I], MULT)
 
         for c in range(T // N_OUT):
             cols = slice(N_OUT * c, N_OUT * (c + 1))

from contextlib import ExitStack

import concourse.mybir as mybir

D, T, I, Q = 512, 1024, 512, 128
FLOPS = 2 * D * T * Q

F32 = mybir.dt.float32
BF16 = mybir.dt.bfloat16
U32 = mybir.dt.uint32
I32 = mybir.dt.int32
U16 = mybir.dt.uint16
U8 = mybir.dt.uint8
FP8X4 = mybir.dt.float8_e4m3fn_x4
FP4X4 = mybir.dt.float4_e2m1fn_x4
MULT = mybir.AluOpType.mult
ADD = mybir.AluOpType.add
COPY = mybir.ActivationFunctionType.Copy

P = 128
PACK = 4
N_MM = 256
HALF = I // 2
N_OUT = 256
LEAD = 128


def tile_attend_pairproduct_lean_timesold_heads_kernel(
    tc, query, keys_words, keys_scales, old, base, offs, offs2, offs3, offs4, out
):
    nc = tc.nc
    with ExitStack() as ctx:
        keep = ctx.enter_context(tc.tile_pool(name="keep", bufs=1))
        psum = ctx.enter_context(tc.psum_pool(name="psum", bufs=1))

        lst1 = keep.tile([P, I // 16], U16, name="lst1")
        lst2 = keep.tile([P, I // 16], U16, name="lst2")
        lst3 = keep.tile([P, I // 16], U16, name="lst3")
        lst4 = keep.tile([P, I // 16], U16, name="lst4")
        q_raw = keep.tile([P, PACK, Q], F32, name="q_raw")
        k_words = keep.tile([P, 2 * T], U8, name="k_words", align_bytes=64)
        k_scales = keep.tile([P, T], U8, name="k_scales", align_bytes=64)
        old_sb = keep.tile([P, T], F32, name="old_sb")
        base_sb = keep.tile([P, T], F32, name="base_sb")
        f1 = keep.tile([P, T], F32, name="f1")
        a_sb = keep.tile([P, T], F32, name="a_sb")

        nc.vector.memset(k_scales[:].bitcast(I32), 0)
        nc.sync.dma_start(q_raw[:], query.rearrange("(p j) q -> p j q", j=PACK))
        nc.sync.dma_start(k_words[:].bitcast(I32), keys_words[0].bitcast(I32))
        for quad in range(4):
            nc.sync.dma_start(
                k_scales[32 * quad : 32 * quad + 4, :].bitcast(I32),
                keys_scales[0, 4 * quad : 4 * quad + 4, :].bitcast(I32),
            )
        nc.sync.dma_start(lst3[:], offs3)
        nc.sync.dma_start(old_sb[:], old)
        nc.sync.dma_start(lst1[:], offs)
        nc.sync.dma_start(lst2[:], offs2)
        nc.sync.dma_start(lst4[:], offs4)
        nc.sync.dma_start(base_sb[:], base)
        nc.vector.memset(f1[:], 0.0)

        q_bf = keep.tile([P, Q, PACK], BF16, name="q_bf", align_bytes=64)
        nc.vector.tensor_copy(
            q_bf[:].rearrange("p (c i) t -> p c t i", i=4),
            q_raw[:].rearrange("p t (c i) -> p c t i", i=4),
        )
        q_codes = keep.tile([P, Q], U32, name="q_codes", align_bytes=64)
        q_scales = keep.tile([P, Q], U8, name="q_scales", align_bytes=64)
        nc.vector.quantize_mx(
            out=q_codes[:].bitcast(FP8X4),
            scales=q_scales[:],
            in_=q_bf[:].rearrange("p c t -> p (c t)"),
        )

        for c in range(T // N_MM):
            bank = psum.tile([P, N_MM], F32, name="bank%d" % c)
            nc.tensor.matmul_mx(
                out=bank[:],
                lhsT=q_codes[:].bitcast(FP8X4),
                lhsT_scale=q_scales[:],
                rhs=k_words[:, 2 * N_MM * c : 2 * N_MM * (c + 1)].bitcast(FP4X4),
                rhs_scale=k_scales[:, N_MM * c : N_MM * (c + 1)],
                start=True,
                stop=True,
            )
            nc.scalar.copy(a_sb[:, N_MM * c : N_MM * (c + 1)], bank[:])

        def slots(lo, hi):
            return slice(lo // 16, hi // 16)

        old_g = keep.tile([P, I], F32, name="old_g")
        a2_g = keep.tile([P, I], F32, name="a2_g")
        a1_g = keep.tile([P, HALF], F32, name="a1_g")
        a1o = keep.tile([P, I], F32, name="a1o")

        for lo in (0, HALF):
            nc.vector.tensor_copy(old_g[:, lo : lo + HALF], old_sb[:].indirect(lst3[:, slots(lo, lo + HALF)]))
        nc.scalar.activation(a2_g[:, 0:HALF], a_sb[:].indirect(lst2[:, slots(0, HALF)]), COPY)
        nc.scalar.activation(a1_g[:], a_sb[:].indirect(lst1[:, slots(HALF, I)]), COPY)
        nc.scalar.activation(a2_g[:, HALF:I], a_sb[:].indirect(lst2[:, slots(HALF, I)]), COPY)
        for lo in (0, LEAD):
            nc.vector.tensor_tensor(
                a1o[:, lo : lo + LEAD], a_sb[:].indirect(lst1[:, slots(lo, lo + LEAD)]), old_g[:, lo : lo + LEAD], MULT
            )
        nc.vector.tensor_tensor(f1[:].indirect(lst4[:, slots(0, LEAD)]), a1o[:, 0:LEAD], a2_g[:, 0:LEAD], MULT)
        nc.vector.tensor_tensor(a1o[:, HALF:I], a1_g[:], old_g[:, HALF:I], MULT)
        nc.vector.tensor_tensor(f1[:].indirect(lst4[:, slots(LEAD, I)]), a1o[:, LEAD:I], a2_g[:, LEAD:I], MULT)

        for c in range(T // N_OUT):
            cols = slice(N_OUT * c, N_OUT * (c + 1))
            res = keep.tile([P, N_OUT], F32, name="res%d" % c)
            nc.vector.tensor_tensor(res[:], base_sb[:, cols], f1[:, cols], ADD)
            queue = nc.sync if c % 2 == 0 else nc.scalar
            queue.dma_start(out[:, cols], res[:])
